import numpy as np
import ml_dtypes

BF16 = ml_dtypes.bfloat16


def bf(x):
    return np.asarray(x, np.float32).astype(BF16)


def f32(x):
    return np.asarray(x, np.float32)


def f64(x):
    return np.asarray(x).astype(np.float64)


def striped(idx):
    return np.tile(idx.reshape(-1, 16).T, (8, 1))


def rows(idx, k):
    return np.tile(idx, (k, 1))


def look(tab, idx):
    return np.take_along_axis(f64(tab), rows(idx, len(tab)), axis=1)


K, S, D, V, N = 128, 2048, 3, 512, 1536


def setup_inputs():
    return {"tab": f32(np.random.standard_normal((K, S))), "u0": f32(np.random.uniform(0.2, 1.0, (K, V))), "u1": f32(np.random.uniform(0.2, 1.0, (K, V))), "u2": f32(np.random.uniform(0.2, 1.0, (K, V))), "offs": striped(np.random.permutation(S)[:N])}


def reference(tab, u0, u1, u2, offs):
    idx = offs[:16].T.reshape(-1)
    x = f64(u0) * np.minimum(np.maximum(look(tab, idx[:V]), -1.25), 1.0) + f64(u1) * np.minimum(np.maximum(look(tab, idx[1 * V:2 * V]), -1.25), 1.0) + f64(u2) * np.minimum(np.maximum(look(tab, idx[2 * V:3 * V]), -1.25), 1.0)
    return x

@@ -1,0 +1,40 @@
+import concourse.mybir as mybir
+
+F32, U16 = mybir.dt.float32, mybir.dt.uint16
+ALU = mybir.AluOpType
+
+P = 128
+V = 512
+D = 3
+LOW, HIGH = -1.25, 1.0
+FLOPS = (4 * D - 1) * P * V
+
+
+def tile_lookup_clipmix_out_kernel(tc, tab, u0, u1, u2, offs, out):
+    nc = tc.nc
+    k = V // 16
+    with tc.tile_pool(name="lists", bufs=1) as lists, tc.tile_pool(name="held", bufs=1) as held:
+        offsets = lists.tile([P, D * k], U16, name="offsets")
+        nc.sync.dma_start(offsets[:], offs)
+        table = held.tile([P, tab.shape[1]], F32, name="table")
+        nc.sync.dma_start(table[:], tab)
+        weights = []
+        for d, u in enumerate((u0, u1, u2)):
+            weight = held.tile([P, V], F32, name=f"weight{d}")
+            nc.sync.dma_start(weight[:], u)
+            weights.append(weight)
+
+        total = None
+        for d in range(D):
+            clamped = held.tile([P, V], F32, name=f"clamped{d}")
+            looked_up = table[:].indirect(offsets[:, d * k : (d + 1) * k])
+            nc.vector.tensor_scalar(clamped[:], looked_up, LOW, HIGH, ALU.max, ALU.min)
+            product = held.tile([P, V], F32, name=f"product{d}")
+            nc.vector.tensor_tensor(product[:], clamped[:], weights[d][:], ALU.mult)
+            if total is None:
+                total = product
+            else:
+                summed = held.tile([P, V], F32, name=f"sum{d}")
+                nc.vector.tensor_tensor(summed[:], total[:], product[:], ALU.add)
+                total = summed
+        nc.sync.dma_start(out, total[:])

@@ -24,17 +24,18 @@ def tile_lookup_clipmix_out_kernel(tc, tab, u0, u1, u2, offs, out):
             nc.sync.dma_start(weight[:], u)
             weights.append(weight)
 
-        total = None
+        products = []
         for d in range(D):
             clamped = held.tile([P, V], F32, name=f"clamped{d}")
             looked_up = table[:].indirect(offsets[:, d * k : (d + 1) * k])
             nc.vector.tensor_scalar(clamped[:], looked_up, LOW, HIGH, ALU.max, ALU.min)
             product = held.tile([P, V], F32, name=f"product{d}")
-            nc.vector.tensor_tensor(product[:], clamped[:], weights[d][:], ALU.mult)
-            if total is None:
-                total = product
-            else:
-                summed = held.tile([P, V], F32, name=f"sum{d}")
-                nc.vector.tensor_tensor(summed[:], total[:], product[:], ALU.add)
-                total = summed
+            multiplier = nc.gpsimd if d < D - 1 else nc.vector
+            multiplier.tensor_tensor(product[:], clamped[:], weights[d][:], ALU.mult)
+            products.append(product)
+
+        first_two = held.tile([P, V], F32, name="first_two")
+        nc.vector.tensor_tensor(first_two[:], products[0][:], products[1][:], ALU.add)
+        total = held.tile([P, V], F32, name="total")
+        nc.vector.tensor_tensor(total[:], first_two[:], products[2][:], ALU.add)
         nc.sync.dma_start(out, total[:])

import concourse.mybir as mybir

F32, U16 = mybir.dt.float32, mybir.dt.uint16
ALU = mybir.AluOpType

P = 128
V = 512
D = 3
LOW, HIGH = -1.25, 1.0
FLOPS = (4 * D - 1) * P * V


def tile_lookup_clipmix_out_kernel(tc, tab, u0, u1, u2, offs, out):
    nc = tc.nc
    k = V // 16
    with tc.tile_pool(name="lists", bufs=1) as lists, tc.tile_pool(name="held", bufs=1) as held:
        offsets = lists.tile([P, D * k], U16, name="offsets")
        nc.sync.dma_start(offsets[:], offs)
        table = held.tile([P, tab.shape[1]], F32, name="table")
        nc.sync.dma_start(table[:], tab)
        weights = []
        for d, u in enumerate((u0, u1, u2)):
            weight = held.tile([P, V], F32, name=f"weight{d}")
            nc.sync.dma_start(weight[:], u)
            weights.append(weight)

        products = []
        for d in range(D):
            clamped = held.tile([P, V], F32, name=f"clamped{d}")
            looked_up = table[:].indirect(offsets[:, d * k : (d + 1) * k])
            nc.vector.tensor_scalar(clamped[:], looked_up, LOW, HIGH, ALU.max, ALU.min)
            product = held.tile([P, V], F32, name=f"product{d}")
            multiplier = nc.gpsimd if d < D - 1 else nc.vector
            multiplier.tensor_tensor(product[:], clamped[:], weights[d][:], ALU.mult)
            products.append(product)

        first_two = held.tile([P, V], F32, name="first_two")
        nc.vector.tensor_tensor(first_two[:], products[0][:], products[1][:], ALU.add)
        total = held.tile([P, V], F32, name="total")
        nc.vector.tensor_tensor(total[:], first_two[:], products[2][:], ALU.add)
        nc.sync.dma_start(out, total[:])
